import numpy as np
import ml_dtypes


def mxq(x, axis, fmt="e4m3"):
    dtype, down = {"e4m3": (ml_dtypes.float8_e4m3fn, 7), "e5m2": (ml_dtypes.float8_e5m2, 14)}[fmt]
    v = np.moveaxis(np.asarray(x, np.float32).astype(ml_dtypes.bfloat16).astype(np.float64), axis, -1)
    blocks = v.reshape(v.shape[:-1] + (-1, 32))
    amax = np.abs(blocks).max(-1, keepdims=True)
    byte = np.maximum(np.where(amax > 0, np.frexp(amax)[1] - 1 + 127, 0) - down, 1)
    scale = np.exp2(byte - 127.0)
    codes = (blocks / scale).astype(np.float32).astype(dtype).astype(np.float64)
    return np.moveaxis((codes * scale).reshape(v.shape), -1, axis)


WIDE = False


def mx_kscale(k):
    if not WIDE:
        return np.ones(k)
    levels = np.array([10, -10, 5, -5, 0])
    if k % 512:
        return np.exp2(np.random.permutation(np.resize(levels, k // 32))).repeat(32)
    a = np.empty((k // 512, 16))
    for p in range(k // 512):
        a[p, :8] = np.random.permutation(np.resize(levels, 8))
        for g in range(8):
            far = levels[np.abs(levels - a[p, g]) >= 10]
            a[p, g + 8] = far[np.random.randint(len(far))]
    return np.exp2(a.ravel()).repeat(32)


def f64(x):
    return np.asarray(x).astype(np.float64)


def striped(idx):
    return np.tile(idx.reshape(-1, 16).T, (8, 1)).astype(np.uint16)


def unstriped(offs):
    return offs[:16].T.reshape(-1).astype(np.int64)


E2M1 = np.array([0.0, 0.5, 1.0, 1.5, 2.0, 3.0, 4.0, 6.0, -0.0, -0.5, -1.0, -1.5, -2.0, -3.0, -4.0, -6.0])


def pack_weight(w, fmt):
    k, n = w.shape
    w = f64(np.asarray(w, np.float32).astype(ml_dtypes.bfloat16)).reshape(k // 32, 32, n)
    amax = np.abs(w).max(1)
    if fmt == "e4m3":
        byte = np.frexp(amax)[1] - 1 + 127 - 7
    else:
        mant, ex = np.frexp(amax / 6.0)
        byte = np.where(mant > 0.5, ex, ex - 1) + 127
    byte = np.clip(np.where(amax > 0, byte, 1), 1, 254)
    scaled = (w * np.exp2(127.0 - byte)[:, None, :]).reshape(k, n).astype(np.float32)
    by_word = np.ascontiguousarray(scaled.reshape(k // 512, 128, 4, n).transpose(0, 1, 3, 2))
    if fmt == "e4m3":
        words = by_word.astype(ml_dtypes.float8_e4m3fn).view(np.uint8)
    else:
        c = by_word.astype(ml_dtypes.float4_e2m1fn).view(np.uint8) & 0xF
        words = (c[..., 0::2] | (c[..., 1::2] << 4)).reshape(k // 512, 128, 2 * n)
    return np.ascontiguousarray(words), np.ascontiguousarray(byte.astype(np.uint8).reshape(k // 512, 16, n))


def unpack_weight(words, scales, fmt):
    g, _, n = scales.shape
    words = np.ascontiguousarray(words).reshape(g, 128, n, -1)
    if fmt == "e4m3":
        vals = words.view(ml_dtypes.float8_e4m3fn).astype(np.float64)
    else:
        nib = np.empty((g, 128, n, 4), np.uint8)
        nib[..., 0::2] = words & 0xF
        nib[..., 1::2] = words >> 4
        vals = E2M1[nib]
    vals = vals * np.repeat(np.exp2(scales.astype(np.float64) - 127.0), 8, axis=1)[..., None]
    return vals.transpose(0, 1, 3, 2).reshape(g * 512, n)


def gelu(v):
    return 0.5 * v * (1.0 + np.tanh(np.sqrt(2.0 / np.pi) * (v + 0.044715 * v**3)))


K, M, TA, TB, S, H, T2, P, N = 1024, 1024, 2048, 1024, 512, 1024, 2048, 1024, 512

def setup_inputs():
    n = np.random.standard_normal
    s, s2, u = mx_kscale(K)[:, None], mx_kscale(M)[:, None], mx_kscale(H)[:, None]
    d = {}
    d["tab_words"], d["tab_scales"] = pack_weight(n((K, TA)) * s, "e4m3")
    d["tab2_words"], d["tab2_scales"] = pack_weight(n((M, TB)) * s2, "e4m3")
    d["offs"] = striped(np.random.permutation(TA)[:S])
    d["offs2"] = striped(np.random.permutation(TB)[:S])
    perm = np.random.permutation(T2)
    d["offs3"] = striped(perm[:S])
    d["offs4"] = striped(perm[S:2 * S])
    d["offs5"] = striped(np.random.permutation(T2)[:P])
    d["w1"] = (1.4 * n((K, H)) / K**0.5 / s * u.T).astype(np.float32)
    d["floors"] = (1.2 * n((H, S)) * u).astype(np.float32)
    d["wc_words"], d["wc_scales"] = pack_weight(0.53 * n((M, H)) / M**0.5 / s2, "e4m3")
    d["wd"] = (1.8 * n((M, H)) / M**0.5 / s2 * u.T).astype(np.float32)
    d["wg1"] = np.exp(0.3 * n((128, S))).astype(np.float32)
    d["wg2"] = np.exp(0.3 * n((128, S))).astype(np.float32)
    d["page0"] = (1.5 * n((H, T2)) * u).astype(np.float32)
    d["wo_words"], d["wo_scales"] = pack_weight(n((H, N)) / H**0.5 / u, "e2m1")
    return d

def reference(tab_words, tab_scales, tab2_words, tab2_scales, offs, offs2, offs3, offs4, offs5,
              w1, floors, wc_words, wc_scales, wd, wg1, wg2, page0, wo_words, wo_scales):
    v = unpack_weight(tab_words, tab_scales, "e4m3")[:, unstriped(offs)]
    v2 = unpack_weight(tab2_words, tab2_scales, "e4m3")[:, unstriped(offs2)]
    h1 = np.maximum(mxq(f64(w1), 0, "e4m3").T @ v, f64(floors))
    phase = unpack_weight(wc_words, wc_scales, "e4m3").T @ v2
    h2 = np.cos(phase) * (mxq(f64(wd), 0, "e4m3").T @ v2)
    page = f64(page0).copy()
    page[:, unstriped(offs3)] = np.tile(f64(wg1), (H // 128, 1)) * h1
    page[:, unstriped(offs4)] = np.tile(f64(wg2), (H // 128, 1)) * h2
    x = page[:, unstriped(offs5)]
    z = mxq(x + np.tanh(x), 0, "e4m3")
    y = unpack_weight(wo_words, wo_scales, "e2m1").T @ z
    return np.sqrt(np.abs(y))

@@ -1,0 +1,360 @@
+import math
+from contextlib import ExitStack
+
+import concourse.mybir as mybir
+from concourse.masks import make_identity
+
+K, TA, TB, S, H, T2, J, N = 1024, 2048, 1024, 512, 1024, 2048, 1024, 512
+FLOPS = 2 * (3 * K * H * S + H * N * J)
+
+F32 = mybir.dt.float32
+BF16 = mybir.dt.bfloat16
+I32 = mybir.dt.int32
+U32 = mybir.dt.uint32
+U16 = mybir.dt.uint16
+U8 = mybir.dt.uint8
+FP8X4 = mybir.dt.float8_e4m3fn_x4
+FP4X4 = mybir.dt.float4_e2m1fn_x4
+ALU = mybir.AluOpType
+ACT = mybir.ActivationFunctionType
+
+P = 128
+PACK = 4
+PASSES = 2
+BANK = 512
+TILES = H // P
+PER_PASS = TILES // PASSES
+HALVES = J // BANK
+CHUNKS = [(0, 1), (1, 3), (3, 5), (5, 7), (7, 8)]
+WC_CHUNKS = [(0, 2), (2, 5), (5, 8)]
+
+
+def tile_list_snail_pen_features_kernel(
+    tc, tab_words, tab_scales, tab2_words, tab2_scales, offs, offs2, offs3, offs4, offs5,
+    w1, floors, wc_words, wc_scales, wd, wg1, wg2, page0, wo_words, wo_scales, out,
+):
+    nc = tc.nc
+    with ExitStack() as ctx:
+        keep = ctx.enter_context(tc.tile_pool(name="keep", bufs=1))
+        ring2 = ctx.enter_context(tc.tile_pool(name="ring2", bufs=2))
+        ring3 = ctx.enter_context(tc.tile_pool(name="ring3", bufs=3))
+        ring4 = ctx.enter_context(tc.tile_pool(name="ring4", bufs=4))
+        psum1 = ctx.enter_context(tc.psum_pool(name="psum1", bufs=1))
+        psum2 = ctx.enter_context(tc.psum_pool(name="psum2", bufs=2))
+
+        def load_list(src, name):
+            t = keep.tile(list(src.shape), U16, name=name)
+            nc.sync.dma_start(out=t[:], in_=src)
+            return t
+
+        def load_words(src, a, name, tag):
+            width = src.shape[2]
+            t = keep.tile([P, width], I32, name=name, tag=tag, align_bytes=64)
+            nc.sync.dma_start(out=t[:], in_=src[a].rearrange("p t i -> p (t i)").bitcast(I32))
+            return t
+
+        def zeroed_plane(width, name):
+            t = keep.tile([P, width], U8, name=name, align_bytes=64)
+            nc.vector.memset(t[:].bitcast(I32), 0)
+            return t
+
+        def load_packed_planes(queue, plane, src):
+            for q in range(4):
+                queue.dma_start(
+                    out=plane[32 * q : 32 * q + 4 * PASSES, :].bitcast(I32),
+                    in_=src[:, 4 * q : 4 * q + 4, :].bitcast(I32),
+                )
+
+        def gather(window, offsets, dtype, name):
+            t = keep.tile([P, S], dtype, name=name, align_bytes=64)
+            nc.vector.tensor_copy(t[:], window[:].bitcast(dtype).indirect(offsets[:]))
+            return t
+
+        tab2_plane = zeroed_plane(TB, "tab2_plane")
+        zero_in = keep.tile([P, 1], F32, name="zero_in")
+        nc.vector.memset(zero_in[:], 0.0)
+        tab_plane = zeroed_plane(TA, "tab_plane")
+        wc_plane = zeroed_plane(H, "wc_plane")
+        wo_plane = zeroed_plane(PASSES * N, "wo_plane")
+        zero = keep.tile([P, 1], F32, name="zero")
+        nc.scalar.activation(zero[:], zero_in[:], ACT.Silu)
+        load_packed_planes(nc.gpsimd, tab_plane, tab_scales)
+        ident = keep.tile([P, P], F32, name="ident")
+        make_identity(nc, ident[:])
+
+        raw = {}
+
+        def load_weight(w, key, chunk):
+            lo, hi = CHUNKS[chunk]
+            t = keep.tile([P, PASSES, PACK, P * (hi - lo)], F32, name="raw", tag="raw_%s%d" % (key, chunk % 2) if chunk < 4 else "raw_last_" + key, align_bytes=64)
+            for a in range(PASSES):
+                rows = w[P * PACK * a : P * PACK * (a + 1), P * lo : P * hi]
+                nc.sync.dma_start(out=t[:, a], in_=rows.rearrange("(p j) c -> p j c", j=PACK))
+            for b in range(lo, hi):
+                raw[key, b] = t[:, :, :, P * (b - lo) : P * (b - lo + 1)]
+
+        wc = {}
+
+        def load_wc(chunk):
+            lo, hi = WC_CHUNKS[chunk]
+            t = keep.tile([P, PASSES, P * (hi - lo)], I32, name="wc%d" % chunk, align_bytes=64)
+            src = wc_words.rearrange("a p c i -> p a (c i)")[:, :, PACK * P * lo : PACK * P * hi]
+            nc.sync.dma_start(out=t[:], in_=src.bitcast(I32))
+            for b in range(lo, hi):
+                wc[b] = t[:, :, P * (b - lo) : P * (b - lo + 1)]
+
+        floor_t, page = {}, {}
+
+        def load_floor(b):
+            floor_t[b] = keep.tile([P, S], F32, name="floor", tag="floor%d" % b)
+            nc.sync.dma_start(out=floor_t[b][:], in_=floors[P * b : P * (b + 1), :])
+
+        def load_page(b):
+            page[b] = keep.tile([P, T2], F32, name="page", tag="wide%d" % b, align_bytes=64)
+            nc.sync.dma_start(out=page[b][:], in_=page0[P * b : P * (b + 1), :])
+
+        def load_gain(src, name):
+            t = keep.tile([P, S], F32, name=name)
+            nc.sync.dma_start(out=t[:], in_=src)
+            return t
+
+        idx2 = load_list(offs2, "idx2")
+        tab2 = [load_words(tab2_words, a, "tab2", "wide%d" % (4 + a)) for a in range(PASSES)]
+        load_packed_planes(nc.sync, tab2_plane, tab2_scales)
+        load_wc(0)
+        tab = [load_words(tab_words, 0, "tab", "wide6")]
+        load_packed_planes(nc.sync, wc_plane, wc_scales)
+        idx = load_list(offs, "idx")
+        tab.append(load_words(tab_words, 1, "tab", "wide7"))
+        load_weight(wd, "wd", 0)
+        load_weight(w1, "w1", 0)
+        load_page(0)
+        idx4 = load_list(offs4, "idx4")
+        gain2 = load_gain(wg2, "gain2")
+        load_floor(0)
+        gain1 = load_gain(wg1, "gain1")
+        idx3 = load_list(offs3, "idx3")
+        load_wc(1)
+        load_weight(wd, "wd", 1)
+        load_weight(w1, "w1", 1)
+        idx5 = load_list(offs5, "idx5")
+        load_page(1)
+        load_floor(1)
+
+        v2 = [gather(tab2[a], idx2, U32, "v2_%d" % a) for a in range(PASSES)]
+        v2_plane = gather(tab2_plane, idx2, U8, "v2_plane")
+        v = [gather(tab[a], idx, U32, "v%d" % a) for a in range(PASSES)]
+        v_plane = gather(tab_plane, idx, U8, "v_plane")
+
+        codes, planes = {}, {}
+
+        def quantize_weights(keys, b):
+            n = len(keys)
+            grouped = keep.tile([P, n, PASSES, P, PACK], BF16, name="grouped", tag="pair%d" % (b % 4) if b > 1 else "first%d%s" % (b, keys[0]), align_bytes=64)
+            for i, key in enumerate(keys):
+                (nc.scalar.copy if b else nc.vector.tensor_copy)(
+                    grouped[:, i].rearrange("p a (c i) t -> p a c t i", i=4),
+                    raw[key, b].rearrange("p a t (c i) -> p a c t i", i=4),
+                )
+            c = keep.tile([P, n * PASSES * P], U32, name="codes", tag="wide%d" % (b - 4) if b >= 4 else "codes%d%s" % (b, keys[0]), align_bytes=64)
+            s = keep.tile([P, n * PASSES * P], U8, name="plane", tag="pair%d" % ((b - 1) % 4) if b >= 5 else "plane%d%s" % (b, keys[0]), align_bytes=64)
+            nc.vector.quantize_mx(out=c[:].bitcast(FP8X4), scales=s[:], in_=grouped[:].rearrange("p n a c t -> p (n a c t)"))
+            for i, key in enumerate(keys):
+                codes[key, b] = c[:, PASSES * P * i : PASSES * P * (i + 1)]
+                planes[key, b] = s[:, PASSES * P * i : PASSES * P * (i + 1)]
+
+        def project(key, b, table, table_plane, tag):
+            acc = psum1.tile([P, BANK], F32, name=tag)
+            for a in range(PASSES):
+                cols = slice(P * a, P * (a + 1))
+                nc.tensor.matmul_mx(
+                    out=acc[:],
+                    lhsT=codes[key, b][:, cols].bitcast(FP8X4),
+                    lhsT_scale=planes[key, b][:, cols],
+                    rhs=table[a][:].bitcast(FP8X4),
+                    rhs_scale=table_plane[4 * a : P, :],
+                    start=(a == 0),
+                    stop=(a == PASSES - 1),
+                )
+            return acc
+
+        h1, h2, cosine = {}, {}, {}
+
+        def make_h1(b):
+            acc = project("w1", b, v, v_plane, "bank_h")
+            h1[b] = keep.tile([P, S], F32, name="h1")
+            nc.vector.tensor_tensor(h1[b][:], acc[:], floor_t[b][:], ALU.max)
+
+        def make_cosine(b):
+            phase = psum1.tile([P, BANK], F32, name="bank_phase")
+            for jt in range(S // P):
+                cols = slice(P * jt, P * (jt + 1))
+                for a in range(PASSES):
+                    nc.tensor.matmul_mx(
+                        out=phase[:, cols],
+                        lhsT=v2[a][:, cols].bitcast(FP8X4),
+                        lhsT_scale=v2_plane[4 * a : P, cols],
+                        rhs=wc[b][:, a, :].bitcast(FP8X4),
+                        rhs_scale=wc_plane[4 * a : P, P * b : P * (b + 1)],
+                        start=(a == 0),
+                        stop=(a == PASSES - 1),
+                    )
+            turns = ring2.tile([P, S], F32, name="turns")[:]
+            shift = ring2.tile([P, S], F32, name="shift")[:]
+            nc.scalar.activation(turns, phase[:], ACT.Abs, bias=zero[:], scale=0.5 / math.pi)
+            whole = ring2.tile([P, S], U32, name="whole")
+            nc.scalar.activation(whole[:], turns, ACT.Copy, bias=0.25)
+            nc.scalar.activation(shift, whole[:], ACT.Copy, bias=0.25, scale=-1.0)
+            rest = psum1.tile([P, BANK], F32, name="bank_rest")
+            for jt in range(S // P):
+                cols = slice(P * jt, P * (jt + 1))
+                for n, term in enumerate((shift, turns)):
+                    nc.tensor.matmul(
+                        rest[:, cols], lhsT=term[:, cols], rhs=ident[:],
+                        start=(n == 0), stop=(n == 1), is_transpose=True,
+                    )
+            cosine[b] = keep.tile([P, S], F32, name="cosine", tag="scratch%d" % (b % 3), align_bytes=64)
+            nc.scalar.activation(cosine[b][:], rest[:], ACT.Sin, bias=zero[:], scale=2.0 * math.pi)
+
+        def make_h2(b):
+            acc = project("wd", b, v2, v2_plane, "bank_d")
+            h2[b] = keep.tile([P, S], F32, name="h2", tag="pair%d" % ((b + 2) % 4 if b > 1 else 2) if b else "first0w1", align_bytes=64)
+            nc.vector.tensor_tensor(h2[b][:], acc[:], cosine[b][:], ALU.mult)
+
+        def put(b, values, gain, offsets):
+            nc.vector.tensor_tensor(page[b][:].indirect(offsets[:]), values[:], gain[:], ALU.mult)
+
+        x = {}
+
+        def fetch(b, pieces):
+            x[b] = keep.tile([P, J], F32, name="x", tag="scratch%d" % ((b + 1) % 3) if b else "first1wd", align_bytes=64)
+            n = J // pieces
+            for i in range(pieces):
+                nc.vector.tensor_copy(
+                    x[b][:, n * i : n * (i + 1)],
+                    page[b][:].indirect(idx5[:, n * i // 16 : n * (i + 1) // 16]),
+                )
+
+        z_rows = {}
+        last_tanh = {}
+
+        def make_z(b, h, copy):
+            a, slot = divmod(b, PER_PASS)
+            if slot == 0:
+                z_rows[a, h] = keep.tile([P, 4, 2, 2 * P], BF16, name="z_rows%d" % h, align_bytes=64)
+            xs = x[b][:, BANK * h : BANK * (h + 1)]
+            if b == 0:
+                th = keep.tile([P, BANK], F32, name="th", tag="raw_%s0" % ("wd", "w1")[h], align_bytes=64)
+            else:
+                th = ring2.tile([P, BANK], F32, name="th")
+            nc.scalar.activation(th[:], xs, ACT.Tanh, bias=zero[:])
+            last_tanh[0] = th
+            zt = psum2.tile([P, 4, P], F32, name="bank_z")
+            for jt in range(4):
+                cols = slice(P * jt, P * (jt + 1))
+                for n, term in enumerate((th, xs)):
+                    nc.tensor.matmul(
+                        zt[:, jt, :], lhsT=term[:, cols], rhs=ident[:],
+                        start=(n == 0), stop=(n == 1), is_transpose=True,
+                    )
+            copy(
+                z_rows[a, h][:, :, :, 64 * slot : 64 * (slot + 1)].rearrange("p j u (q e) -> p j u q e", e=2),
+                zt[:].rearrange("p j (q u e) -> p j u q e", u=2, e=2),
+            )
+
+        z_codes, z_plane = {}, {}
+
+        def quantize_z(a, h, copies):
+            grouped = keep.tile([P, BANK * PACK], BF16, name="grouped_z", tag="raw_last_" + ("wd", "w1")[h], align_bytes=64)
+            words = grouped[:].bitcast(F32)
+            for k in range(2):
+                bank = psum2.tile([P, 2, 2, P], F32, name="bank_w")
+                for i in range(2):
+                    for u in range(2):
+                        nc.tensor.transpose(bank[:, i, u, :], z_rows[a, h][:, 2 * k + i, u, :].bitcast(F32), ident[:])
+                copies[k](
+                    words[:, BANK * k : BANK * (k + 1)].rearrange("p (i j u) -> p i j u", i=2, u=2),
+                    bank[:].rearrange("p i u j -> p i j u"),
+                )
+            z_codes[a, h] = keep.tile([P, BANK], U32, name="z_codes%d%d" % (a, h), align_bytes=64)
+            z_plane[a, h] = keep.tile([P, BANK], U8, name="z_plane%d%d" % (a, h), align_bytes=64)
+            nc.vector.quantize_mx(out=z_codes[a, h][:].bitcast(FP8X4), scales=z_plane[a, h][:], in_=grouped[:])
+
+        def finish(h, nt, on_vector):
+            acc = psum1.tile([P, BANK], F32, name=("bank_h", "bank_d", "bank_phase", "bank_rest")[nt])
+            for a in range(PASSES):
+                nc.tensor.matmul_mx(
+                    out=acc[:],
+                    lhsT=wo[:, a, 2 * P * nt : 2 * P * (nt + 1)].bitcast(FP4X4),
+                    lhsT_scale=wo_plane[:, N * a + P * nt : N * a + P * (nt + 1)],
+                    rhs=z_codes[a, h][:].bitcast(FP8X4),
+                    rhs_scale=z_plane[a, h][:],
+                    start=(a == 0),
+                    stop=(a == PASSES - 1),
+                )
+            size = ring2.tile([P, BANK], F32, name="size", tag="turns" if on_vector else "shift")
+            if on_vector:
+                minus = ring2.tile([P, BANK], F32, name="minus", tag="th")
+                nc.vector.tensor_scalar(minus[:], acc[:], -1.0, None, ALU.mult)
+                nc.vector.tensor_tensor(size[:], acc[:], minus[:], ALU.max)
+            else:
+                nc.scalar.activation(size[:], acc[:], ACT.Abs, bias=zero[:])
+            root = keep.tile([P, BANK], F32, name="root", tag="floor%d" % (4 * h + nt))
+            nc.scalar.activation(root[:], size[:], ACT.Sqrt, bias=zero_root[:])
+            nc.sync.dma_start(out=out[P * nt : P * (nt + 1), BANK * h : BANK * (h + 1)], in_=root[:])
+
+        make_cosine(0)
+        quantize_weights(["wd"], 0)
+        quantize_weights(["w1"], 0)
+        make_h2(0)
+        make_h1(0)
+        make_cosine(1)
+        quantize_weights(["wd", "w1"], 1)
+
+        for chunk in range(2, len(CHUNKS)):
+            load_weight(wd, "wd", chunk)
+            load_weight(w1, "w1", chunk)
+            if chunk == 2:
+                load_wc(2)
+        for b in range(2, TILES):
+            load_page(b)
+            load_floor(b)
+        wo = keep.tile([P, PASSES, 2 * N], U8, name="wo", align_bytes=64)
+        nc.sync.dma_start(out=wo[:].bitcast(I32), in_=wo_words.rearrange("a p c -> p a c").bitcast(I32))
+        for q in range(4):
+            nc.sync.dma_start(
+                out=wo_plane[32 * q : 32 * q + 4, :].bitcast(I32).rearrange("p (a n) -> p a n", a=PASSES),
+                in_=wo_scales[:, 4 * q : 4 * q + 4, :].rearrange("a r n -> r a n").bitcast(I32),
+            )
+
+        on_scalar, on_vector = nc.scalar.copy, nc.vector.tensor_copy
+        for b in range(TILES):
+            last = b == TILES - 1
+            put(b, h2[b], gain2, idx4)
+            if b == 0:
+                quantize_weights(["wd", "w1"], 2)
+            if b + 3 < TILES:
+                quantize_weights(["wd", "w1"], b + 3)
+            if b == PER_PASS:
+                for h in range(HALVES):
+                    quantize_z(0, h, (on_scalar, on_scalar))
+            put(b, h1[b], gain1, idx3)
+            if b == 0:
+                fetch(b, 1)
+            if not last:
+                make_h2(b + 1)
+                make_h1(b + 1)
+            if b + 2 < TILES:
+                make_cosine(b + 2)
+            if b > 0:
+                fetch(b, HALVES if last else 1)
+            for h in range(HALVES):
+                make_z(b, h, on_vector if last else on_scalar)
+            if last:
+                zero_root = keep.tile([P, 1], F32, name="zero_root")
+                nc.scalar.activation(zero_root[:], last_tanh[0][:, :1], ACT.Sqrt, bias=zero[:], scale=0.0)
+        for h in range(HALVES):
+            quantize_z(1, h, (on_vector, on_scalar))
+        for h in range(HALVES):
+            for nt in range(N // P):
+                finish(h, nt, nt % 2 == 1)

@@ -25,8 +25,8 @@ BANK = 512
 TILES = H // P
 PER_PASS = TILES // PASSES
 HALVES = J // BANK
-CHUNKS = [(0, 1), (1, 3), (3, 5), (5, 7), (7, 8)]
-WC_CHUNKS = [(0, 2), (2, 5), (5, 8)]
+CHUNKS = [(0, 1), (1, 2), (2, 4), (4, 6), (6, 8)]
+WC_CHUNKS = [(0, 3), (3, 8)]
 
 
 def tile_list_snail_pen_features_kernel(
@@ -86,7 +86,7 @@ def tile_list_snail_pen_features_kernel(
 
         def load_weight(w, key, chunk):
             lo, hi = CHUNKS[chunk]
-            t = keep.tile([P, PASSES, PACK, P * (hi - lo)], F32, name="raw", tag="raw_%s%d" % (key, chunk % 2) if chunk < 4 else "raw_last_" + key, align_bytes=64)
+            t = keep.tile([P, PASSES, PACK, P * (hi - lo)], F32, name="raw", tag="raw_%s%d" % (key, chunk % 2 if chunk < 4 else 2), align_bytes=64)
             for a in range(PASSES):
                 rows = w[P * PACK * a : P * PACK * (a + 1), P * lo : P * hi]
                 nc.sync.dma_start(out=t[:, a], in_=rows.rearrange("(p j) c -> p j c", j=PACK))
@@ -106,7 +106,7 @@ def tile_list_snail_pen_features_kernel(
         floor_t, page = {}, {}
 
         def load_floor(b):
-            floor_t[b] = keep.tile([P, S], F32, name="floor", tag="floor%d" % b)
+            floor_t[b] = keep.tile([P, S], F32, name="floor", tag="floor%d" % b, align_bytes=64)
             nc.sync.dma_start(out=floor_t[b][:], in_=floors[P * b : P * (b + 1), :])
 
         def load_page(b):
@@ -131,15 +131,12 @@ def tile_list_snail_pen_features_kernel(
         load_page(0)
         idx4 = load_list(offs4, "idx4")
         gain2 = load_gain(wg2, "gain2")
+        load_weight(wd, "wd", 1)
         load_floor(0)
         gain1 = load_gain(wg1, "gain1")
         idx3 = load_list(offs3, "idx3")
-        load_wc(1)
-        load_weight(wd, "wd", 1)
         load_weight(w1, "w1", 1)
         idx5 = load_list(offs5, "idx5")
-        load_page(1)
-        load_floor(1)
 
         v2 = [gather(tab2[a], idx2, U32, "v2_%d" % a) for a in range(PASSES)]
         v2_plane = gather(tab2_plane, idx2, U8, "v2_plane")
@@ -148,20 +145,25 @@ def tile_list_snail_pen_features_kernel(
 
         codes, planes = {}, {}
 
-        def quantize_weights(keys, b):
-            n = len(keys)
-            grouped = keep.tile([P, n, PASSES, P, PACK], BF16, name="grouped", tag="pair%d" % (b % 4) if b > 1 else "first%d%s" % (b, keys[0]), align_bytes=64)
-            for i, key in enumerate(keys):
-                (nc.scalar.copy if b else nc.vector.tensor_copy)(
-                    grouped[:, i].rearrange("p a (c i) t -> p a c t i", i=4),
-                    raw[key, b].rearrange("p a t (c i) -> p a c t i", i=4),
-                )
-            c = keep.tile([P, n * PASSES * P], U32, name="codes", tag="wide%d" % (b - 4) if b >= 4 else "codes%d%s" % (b, keys[0]), align_bytes=64)
-            s = keep.tile([P, n * PASSES * P], U8, name="plane", tag="pair%d" % ((b - 1) % 4) if b >= 5 else "plane%d%s" % (b, keys[0]), align_bytes=64)
-            nc.vector.quantize_mx(out=c[:].bitcast(FP8X4), scales=s[:], in_=grouped[:].rearrange("p n a c t -> p (n a c t)"))
-            for i, key in enumerate(keys):
-                codes[key, b] = c[:, PASSES * P * i : PASSES * P * (i + 1)]
-                planes[key, b] = s[:, PASSES * P * i : PASSES * P * (i + 1)]
+        grouped = {}
+
+        def round_weight(key, b, copy):
+            grouped[key, b] = keep.tile(
+                [P, PASSES, P, PACK], BF16, name="grouped", tag="grouped_%s%d" % (key, b % 3), align_bytes=64
+            )
+            copy(
+                grouped[key, b][:].rearrange("p a (c i) t -> p a c t i", i=4),
+                raw[key, b].rearrange("p a t (c i) -> p a c t i", i=4),
+            )
+
+        def quantize_weight(key, b, after):
+            codes[key, b] = ring3.tile([P, PASSES * P], U32, name="codes_" + key, align_bytes=64)
+            planes[key, b] = keep.tile([P, PASSES * P], U8, name="plane", tag=after, align_bytes=64)
+            nc.vector.quantize_mx(
+                out=codes[key, b][:].bitcast(FP8X4),
+                scales=planes[key, b][:],
+                in_=grouped[key, b][:].rearrange("p a c t -> p (a c t)"),
+            )
 
         def project(key, b, table, table_plane, tag):
             acc = psum1.tile([P, BANK], F32, name=tag)
@@ -178,12 +180,28 @@ def tile_list_snail_pen_features_kernel(
                 )
             return acc
 
-        h1, h2, cosine = {}, {}, {}
+        h1_sum, h1, h2, cosine = {}, {}, {}, {}
+
+        def h1_tag(b):
+            return "wide%d" % (b - 1) if b else "h1_first"
+
+        def h2_tag(b):
+            return "grouped_wd%d" % ((b + 1) % 3) if b > 1 else ("grouped_w10", "h2_first")[b]
 
         def make_h1(b):
-            acc = project("w1", b, v, v_plane, "bank_h")
-            h1[b] = keep.tile([P, S], F32, name="h1")
+            acc = h1_sum[b]
+            h1[b] = keep.tile([P, S], F32, name="h1", tag=h1_tag(b), align_bytes=64)
             nc.vector.tensor_tensor(h1[b][:], acc[:], floor_t[b][:], ALU.max)
+
+        def add_transposed(bank, first, second):
+            blocks = BANK // P
+            for n, term in enumerate((first, second)):
+                for jt in range(blocks):
+                    cols = slice(P * jt, P * (jt + 1))
+                    nc.tensor.matmul(
+                        bank[:, cols], lhsT=term[:, cols], rhs=ident[:], is_transpose=True,
+                        start=(n == 0 and jt == 0), stop=(n == 1 and jt == blocks - 1),
+                    )
 
         def make_cosine(b):
             phase = psum1.tile([P, BANK], F32, name="bank_phase")
@@ -206,34 +224,25 @@ def tile_list_snail_pen_features_kernel(
             nc.scalar.activation(whole[:], turns, ACT.Copy, bias=0.25)
             nc.scalar.activation(shift, whole[:], ACT.Copy, bias=0.25, scale=-1.0)
             rest = psum1.tile([P, BANK], F32, name="bank_rest")
-            for jt in range(S // P):
-                cols = slice(P * jt, P * (jt + 1))
-                for n, term in enumerate((shift, turns)):
-                    nc.tensor.matmul(
-                        rest[:, cols], lhsT=term[:, cols], rhs=ident[:],
-                        start=(n == 0), stop=(n == 1), is_transpose=True,
-                    )
-            cosine[b] = keep.tile([P, S], F32, name="cosine", tag="scratch%d" % (b % 3), align_bytes=64)
-            nc.scalar.activation(cosine[b][:], rest[:], ACT.Sin, bias=zero[:], scale=2.0 * math.pi)
+            add_transposed(rest[:], turns, shift)
+            cosine[b] = keep.tile([P, S], F32, name="cosine", tag="scratch%d" % (b % 3), align_bytes=64)[:]
+            nc.scalar.activation(cosine[b], rest[:], ACT.Sin, bias=zero[:], scale=2.0 * math.pi)
 
         def make_h2(b):
             acc = project("wd", b, v2, v2_plane, "bank_d")
-            h2[b] = keep.tile([P, S], F32, name="h2", tag="pair%d" % ((b + 2) % 4 if b > 1 else 2) if b else "first0w1", align_bytes=64)
-            nc.vector.tensor_tensor(h2[b][:], acc[:], cosine[b][:], ALU.mult)
+            h2[b] = keep.tile([P, S], F32, name="h2", tag=h2_tag(b), align_bytes=64)
+            nc.vector.tensor_tensor(h2[b][:], acc[:], cosine[b], ALU.mult)
 
         def put(b, values, gain, offsets):
             nc.vector.tensor_tensor(page[b][:].indirect(offsets[:]), values[:], gain[:], ALU.mult)
 
         x = {}
 
-        def fetch(b, pieces):
-            x[b] = keep.tile([P, J], F32, name="x", tag="scratch%d" % ((b + 1) % 3) if b else "first1wd", align_bytes=64)
-            n = J // pieces
-            for i in range(pieces):
-                nc.vector.tensor_copy(
-                    x[b][:, n * i : n * (i + 1)],
-                    page[b][:].indirect(idx5[:, n * i // 16 : n * (i + 1) // 16]),
-                )
+        def fetch(b, h0, h1, tag):
+            t = keep.tile([P, BANK * (h1 - h0)], F32, name="x", tag=tag, align_bytes=64)
+            nc.vector.tensor_copy(t[:], page[b][:].indirect(idx5[:, BANK * h0 // 16 : BANK * h1 // 16]))
+            for h in range(h0, h1):
+                x[b, h] = t[:, BANK * (h - h0) : BANK * (h - h0 + 1)]
 
         z_rows = {}
         last_tanh = {}
@@ -242,21 +251,15 @@ def tile_list_snail_pen_features_kernel(
             a, slot = divmod(b, PER_PASS)
             if slot == 0:
                 z_rows[a, h] = keep.tile([P, 4, 2, 2 * P], BF16, name="z_rows%d" % h, align_bytes=64)
-            xs = x[b][:, BANK * h : BANK * (h + 1)]
+            xs = x[b, h]
             if b == 0:
-                th = keep.tile([P, BANK], F32, name="th", tag="raw_%s0" % ("wd", "w1")[h], align_bytes=64)
+                th = keep.tile([P, BANK], F32, name="th", tag="raw_wd0", align_bytes=64)
             else:
                 th = ring2.tile([P, BANK], F32, name="th")
             nc.scalar.activation(th[:], xs, ACT.Tanh, bias=zero[:])
             last_tanh[0] = th
             zt = psum2.tile([P, 4, P], F32, name="bank_z")
-            for jt in range(4):
-                cols = slice(P * jt, P * (jt + 1))
-                for n, term in enumerate((th, xs)):
-                    nc.tensor.matmul(
-                        zt[:, jt, :], lhsT=term[:, cols], rhs=ident[:],
-                        start=(n == 0), stop=(n == 1), is_transpose=True,
-                    )
+            add_transposed(zt[:].rearrange("p j r -> p (j r)"), xs, th[:])
             copy(
                 z_rows[a, h][:, :, :, 64 * slot : 64 * (slot + 1)].rearrange("p j u (q e) -> p j u q e", e=2),
                 zt[:].rearrange("p j (q u e) -> p j u q e", u=2, e=2),
@@ -264,11 +267,13 @@ def tile_list_snail_pen_features_kernel(
 
         z_codes, z_plane = {}, {}
 
-        def quantize_z(a, h, copies):
-            grouped = keep.tile([P, BANK * PACK], BF16, name="grouped_z", tag="raw_last_" + ("wd", "w1")[h], align_bytes=64)
-            words = grouped[:].bitcast(F32)
+        z_grouped = {}
+
+        def group_z(a, h, copies):
+            z_grouped[a, h] = ring2.tile([P, BANK * PACK], BF16, name="grouped_z", align_bytes=64)
+            words = z_grouped[a, h][:].bitcast(F32)
             for k in range(2):
-                bank = psum2.tile([P, 2, 2, P], F32, name="bank_w")
+                bank = psum2.tile([P, 2, 2, P], F32, name="bank_z" if (a, h) == (1, 1) else "bank_w")
                 for i in range(2):
                     for u in range(2):
                         nc.tensor.transpose(bank[:, i, u, :], z_rows[a, h][:, 2 * k + i, u, :].bitcast(F32), ident[:])
@@ -276,12 +281,17 @@ def tile_list_snail_pen_features_kernel(
                     words[:, BANK * k : BANK * (k + 1)].rearrange("p (i j u) -> p i j u", i=2, u=2),
                     bank[:].rearrange("p i u j -> p i j u"),
                 )
-            z_codes[a, h] = keep.tile([P, BANK], U32, name="z_codes%d%d" % (a, h), align_bytes=64)
+
+        def quantize_z(a, h, tag):
+            z_codes[a, h] = keep.tile([P, BANK], U32, name="z_codes", tag=tag, align_bytes=64)
             z_plane[a, h] = keep.tile([P, BANK], U8, name="z_plane%d%d" % (a, h), align_bytes=64)
-            nc.vector.quantize_mx(out=z_codes[a, h][:].bitcast(FP8X4), scales=z_plane[a, h][:], in_=grouped[:])
+            nc.vector.quantize_mx(out=z_codes[a, h][:].bitcast(FP8X4), scales=z_plane[a, h][:], in_=z_grouped[a, h][:])
 
         def finish(h, nt, on_vector):
-            acc = psum1.tile([P, BANK], F32, name=("bank_h", "bank_d", "bank_phase", "bank_rest")[nt])
+            if nt < 2:
+                acc = psum1.tile([P, BANK], F32, name=(("bank_phase", "bank_rest"), ("bank_d", "bank_h"))[h][nt])
+            else:
+                acc = psum2.tile([P, BANK], F32, name=("bank_w", "bank_z")[h])
             for a in range(PASSES):
                 nc.tensor.matmul_mx(
                     out=acc[:],
@@ -292,31 +302,35 @@ def tile_list_snail_pen_features_kernel(
                     start=(a == 0),
                     stop=(a == PASSES - 1),
                 )
-            size = ring2.tile([P, BANK], F32, name="size", tag="turns" if on_vector else "shift")
+            size = ring2.tile([P, BANK], F32, name="size", tag="turns" if on_vector else "whole")
             if on_vector:
                 minus = ring2.tile([P, BANK], F32, name="minus", tag="th")
                 nc.vector.tensor_scalar(minus[:], acc[:], -1.0, None, ALU.mult)
                 nc.vector.tensor_tensor(size[:], acc[:], minus[:], ALU.max)
             else:
                 nc.scalar.activation(size[:], acc[:], ACT.Abs, bias=zero[:])
-            root = keep.tile([P, BANK], F32, name="root", tag="floor%d" % (4 * h + nt))
+            root = keep.tile([P, BANK], F32, name="root", tag="floor%d" % (4 * h + nt), align_bytes=64)
             nc.scalar.activation(root[:], size[:], ACT.Sqrt, bias=zero_root[:])
             nc.sync.dma_start(out=out[P * nt : P * (nt + 1), BANK * h : BANK * (h + 1)], in_=root[:])
 
+        on_scalar, on_vector = nc.scalar.copy, nc.vector.tensor_copy
         make_cosine(0)
-        quantize_weights(["wd"], 0)
-        quantize_weights(["w1"], 0)
+        for key in ("wd", "w1"):
+            round_weight(key, 0, on_vector)
+            quantize_weight(key, 0, "plane_first_" + key)
         make_h2(0)
-        make_h1(0)
+        h1_sum[0] = project("w1", 0, v, v_plane, "bank_h")
         make_cosine(1)
-        quantize_weights(["wd", "w1"], 1)
+        round_weight("wd", 1, on_scalar)
 
         for chunk in range(2, len(CHUNKS)):
             load_weight(wd, "wd", chunk)
             load_weight(w1, "w1", chunk)
             if chunk == 2:
-                load_wc(2)
-        for b in range(2, TILES):
+                load_wc(1)
+            load_page(chunk - 1)
+            load_floor(chunk - 1)
+        for b in range(len(CHUNKS) - 1, TILES):
             load_page(b)
             load_floor(b)
         wo = keep.tile([P, PASSES, 2 * N], U8, name="wo", align_bytes=64)
@@ -327,34 +341,45 @@ def tile_list_snail_pen_features_kernel(
                 in_=wo_scales[:, 4 * q : 4 * q + 4, :].rearrange("a r n -> r a n").bitcast(I32),
             )
 
-        on_scalar, on_vector = nc.scalar.copy, nc.vector.tensor_copy
         for b in range(TILES):
             last = b == TILES - 1
             put(b, h2[b], gain2, idx4)
-            if b == 0:
-                quantize_weights(["wd", "w1"], 2)
-            if b + 3 < TILES:
-                quantize_weights(["wd", "w1"], b + 3)
-            if b == PER_PASS:
-                for h in range(HALVES):
-                    quantize_z(0, h, (on_scalar, on_scalar))
+            make_h1(b)
+            if b < 2:
+                quantize_weight("wd", b + 1, h2_tag(b))
+            if b == 1:
+                quantize_weight("wd", 3, "floor1")
+            if 2 <= b < TILES - 2:
+                quantize_weight("wd", b + 2, h2_tag(b))
+            if b >= TILES - HALVES:
+                quantize_z(0, b - (TILES - HALVES), h2_tag(b))
             put(b, h1[b], gain1, idx3)
-            if b == 0:
-                fetch(b, 1)
             if not last:
                 make_h2(b + 1)
-                make_h1(b + 1)
+                round_weight("w1", b + 1, on_scalar)
+                quantize_weight("w1", b + 1, h1_tag(b))
+                h1_sum[b + 1] = project("w1", b + 1, v, v_plane, "bank_h")
+            if b == 0:
+                round_weight("wd", 2, on_scalar)
+            if b + 3 < TILES:
+                round_weight("wd", b + 3, on_scalar)
             if b + 2 < TILES:
                 make_cosine(b + 2)
-            if b > 0:
-                fetch(b, HALVES if last else 1)
+            if b == PER_PASS:
+                for h in range(HALVES):
+                    group_z(0, h, (on_scalar, on_scalar))
+            if last:
+                fetch(b, 0, 1, "scratch0")
+                fetch(b, 1, 2, "scratch2")
+            else:
+                fetch(b, 0, 2, "scratch%d" % ((b + 1) % 3) if b > 1 else "grouped_w1%d" % (b + 1))
             for h in range(HALVES):
                 make_z(b, h, on_vector if last else on_scalar)
-            if last:
-                zero_root = keep.tile([P, 1], F32, name="zero_root")
-                nc.scalar.activation(zero_root[:], last_tanh[0][:, :1], ACT.Sqrt, bias=zero[:], scale=0.0)
+        zero_root = keep.tile([P, 1], F32, name="zero_root")
+        nc.scalar.activation(zero_root[:], last_tanh[0][:, :1], ACT.Sqrt, bias=zero[:], scale=0.0)
         for h in range(HALVES):
-            quantize_z(1, h, (on_vector, on_scalar))
+            group_z(1, h, (on_vector, on_scalar))
+            quantize_z(1, h, "wide%d" % h)
         for h in range(HALVES):
             for nt in range(N // P):
-                finish(h, nt, nt % 2 == 1)
+                finish(h, nt, (h, nt) in {(0, 2), (0, 3), (1, 0), (1, 2)})

@@ -71,14 +71,14 @@ def tile_list_snail_pen_features_kernel(
             return t
 
         tab2_plane = zeroed_plane(TB, "tab2_plane")
+        wc_plane = zeroed_plane(H, "wc_plane")
         zero_in = keep.tile([P, 1], F32, name="zero_in")
         nc.vector.memset(zero_in[:], 0.0)
         tab_plane = zeroed_plane(TA, "tab_plane")
-        wc_plane = zeroed_plane(H, "wc_plane")
         wo_plane = zeroed_plane(PASSES * N, "wo_plane")
         zero = keep.tile([P, 1], F32, name="zero")
         nc.scalar.activation(zero[:], zero_in[:], ACT.Silu)
-        load_packed_planes(nc.gpsimd, tab_plane, tab_scales)
+        load_packed_planes(nc.gpsimd, wc_plane, wc_scales)
         ident = keep.tile([P, P], F32, name="ident")
         make_identity(nc, ident[:])
 
@@ -123,7 +123,7 @@ def tile_list_snail_pen_features_kernel(
         load_packed_planes(nc.sync, tab2_plane, tab2_scales)
         load_wc(0)
         tab = [load_words(tab_words, 0, "tab", "wide6")]
-        load_packed_planes(nc.sync, wc_plane, wc_scales)
+        load_packed_planes(nc.sync, tab_plane, tab_scales)
         idx = load_list(offs, "idx")
         tab.append(load_words(tab_words, 1, "tab", "wide7"))
         load_weight(wd, "wd", 0)
@@ -310,8 +310,11 @@ def tile_list_snail_pen_features_kernel(
             else:
                 nc.scalar.activation(size[:], acc[:], ACT.Abs, bias=zero[:])
             root = keep.tile([P, BANK], F32, name="root", tag="floor%d" % (4 * h + nt), align_bytes=64)
-            nc.scalar.activation(root[:], size[:], ACT.Sqrt, bias=zero_root[:])
-            nc.sync.dma_start(out=out[P * nt : P * (nt + 1), BANK * h : BANK * (h + 1)], in_=root[:])
+            pieces = 2 if (h, nt) == (HALVES - 1, N // P - 1) else 1
+            for i in range(pieces):
+                lo, hi = BANK * i // pieces, BANK * (i + 1) // pieces
+                nc.scalar.activation(root[:, lo:hi], size[:, lo:hi], ACT.Sqrt, bias=zero_root[:])
+                nc.sync.dma_start(out=out[P * nt : P * (nt + 1), BANK * h + lo : BANK * h + hi], in_=root[:, lo:hi])
 
         on_scalar, on_vector = nc.scalar.copy, nc.vector.tensor_copy
         make_cosine(0)
@@ -322,14 +325,15 @@ def tile_list_snail_pen_features_kernel(
         h1_sum[0] = project("w1", 0, v, v_plane, "bank_h")
         make_cosine(1)
         round_weight("wd", 1, on_scalar)
+        round_weight("w1", 1, on_scalar)
 
         for chunk in range(2, len(CHUNKS)):
             load_weight(wd, "wd", chunk)
             load_weight(w1, "w1", chunk)
-            if chunk == 2:
-                load_wc(1)
             load_page(chunk - 1)
             load_floor(chunk - 1)
+            if chunk == 2:
+                load_wc(1)
         for b in range(len(CHUNKS) - 1, TILES):
             load_page(b)
             load_floor(b)
@@ -356,7 +360,6 @@ def tile_list_snail_pen_features_kernel(
             put(b, h1[b], gain1, idx3)
             if not last:
                 make_h2(b + 1)
-                round_weight("w1", b + 1, on_scalar)
                 quantize_weight("w1", b + 1, h1_tag(b))
                 h1_sum[b + 1] = project("w1", b + 1, v, v_plane, "bank_h")
             if b == 0:
@@ -364,6 +367,7 @@ def tile_list_snail_pen_features_kernel(
             if b + 3 < TILES:
                 round_weight("wd", b + 3, on_scalar)
             if b + 2 < TILES:
+                round_weight("w1", b + 2, on_scalar)
                 make_cosine(b + 2)
             if b == PER_PASS:
                 for h in range(HALVES):

@@ -22,11 +22,15 @@ P = 128
 PACK = 4
 PASSES = 2
 BANK = 512
+LIST_ROWS = 16
 TILES = H // P
 PER_PASS = TILES // PASSES
 HALVES = J // BANK
-CHUNKS = [(0, 1), (1, 2), (2, 4), (4, 6), (6, 8)]
-WC_CHUNKS = [(0, 3), (3, 8)]
+PIECE = 256
+PIECES = J // PIECE
+DEPTH = 3
+WEIGHT_LOADS = [(0, 1), (1, 2), (2, 4), (4, 6), (6, 8)]
+WC_LOADS = [(0, DEPTH), (DEPTH, TILES)]
 
 
 def tile_list_snail_pen_features_kernel(
@@ -37,38 +41,73 @@ def tile_list_snail_pen_features_kernel(
     with ExitStack() as ctx:
         keep = ctx.enter_context(tc.tile_pool(name="keep", bufs=1))
         ring2 = ctx.enter_context(tc.tile_pool(name="ring2", bufs=2))
-        ring3 = ctx.enter_context(tc.tile_pool(name="ring3", bufs=3))
-        ring4 = ctx.enter_context(tc.tile_pool(name="ring4", bufs=4))
+        ring3 = ctx.enter_context(tc.tile_pool(name="ring3", bufs=DEPTH))
         psum1 = ctx.enter_context(tc.psum_pool(name="psum1", bufs=1))
         psum2 = ctx.enter_context(tc.psum_pool(name="psum2", bufs=2))
+        on_scalar, on_vector = nc.scalar.copy, nc.vector.tensor_copy
+
+        def held(shape, dtype, buffer):
+            return keep.tile(shape, dtype, name=buffer, align_bytes=64)
 
         def load_list(src, name):
-            t = keep.tile(list(src.shape), U16, name=name)
-            nc.sync.dma_start(out=t[:], in_=src)
-            return t
+            offsets = keep.tile(list(src.shape), U16, name=name)
+            nc.sync.dma_start(out=offsets[:], in_=src)
+            return offsets
 
-        def load_words(src, a, name, tag):
-            width = src.shape[2]
-            t = keep.tile([P, width], I32, name=name, tag=tag, align_bytes=64)
-            nc.sync.dma_start(out=t[:], in_=src[a].rearrange("p t i -> p (t i)").bitcast(I32))
-            return t
+        def load_words(src, a, buffer):
+            words = held([P, src.shape[2]], I32, buffer)
+            nc.sync.dma_start(out=words[:], in_=src[a].rearrange("p t i -> p (t i)").bitcast(I32))
+            return words
 
-        def zeroed_plane(width, name):
-            t = keep.tile([P, width], U8, name=name, align_bytes=64)
-            nc.vector.memset(t[:].bitcast(I32), 0)
-            return t
+        def zeroed_plane(width, buffer):
+            plane = held([P, width], U8, buffer)
+            nc.vector.memset(plane[:].bitcast(I32), 0)
+            return plane
 
-        def load_packed_planes(queue, plane, src):
+        def load_shared_plane(queue, plane, src):
             for q in range(4):
                 queue.dma_start(
                     out=plane[32 * q : 32 * q + 4 * PASSES, :].bitcast(I32),
                     in_=src[:, 4 * q : 4 * q + 4, :].bitcast(I32),
                 )
 
-        def gather(window, offsets, dtype, name):
-            t = keep.tile([P, S], dtype, name=name, align_bytes=64)
-            nc.vector.tensor_copy(t[:], window[:].bitcast(dtype).indirect(offsets[:]))
-            return t
+        raw, wc, floor, page = {}, {}, {}, {}
+
+        def load_weight(key, load):
+            lo, hi = WEIGHT_LOADS[load]
+            slot = load % 2 if load < len(WEIGHT_LOADS) - 1 else 2
+            staged = held([P, PASSES, PACK, P * (hi - lo)], F32, "raw_%s%d" % (key, slot))
+            for a in range(PASSES):
+                rows = {"w1": w1, "wd": wd}[key][P * PACK * a : P * PACK * (a + 1), P * lo : P * hi]
+                nc.sync.dma_start(out=staged[:, a], in_=rows.rearrange("(p t) c -> p t c", t=PACK))
+            for b in range(lo, hi):
+                raw[key, b] = staged[:, :, :, P * (b - lo) : P * (b - lo + 1)]
+
+        def load_wc(load):
+            lo, hi = WC_LOADS[load]
+            words = held([P, PASSES, P * (hi - lo)], I32, "wc%d" % load)
+            src = wc_words.rearrange("a p c i -> p a (c i)")[:, :, PACK * P * lo : PACK * P * hi]
+            nc.sync.dma_start(out=words[:], in_=src.bitcast(I32))
+            for b in range(lo, hi):
+                wc[b] = words[:, :, P * (b - lo) : P * (b - lo + 1)]
+
+        def load_floor(b):
+            floor[b] = held([P, S], F32, "floor%d" % b)
+            nc.sync.dma_start(out=floor[b][:], in_=floors[P * b : P * (b + 1), :])
+
+        def load_page(b):
+            page[b] = held([P, T2], F32, "wide%d" % b)
+            nc.sync.dma_start(out=page[b][:], in_=page0[P * b : P * (b + 1), :])
+
+        def load_gain(src, name):
+            gain = keep.tile([P, S], F32, name=name)
+            nc.sync.dma_start(out=gain[:], in_=src)
+            return gain
+
+        def gather_table(window, offsets, dtype, buffer):
+            picked = held([P, S], dtype, buffer)
+            nc.vector.tensor_copy(picked[:], window[:].bitcast(dtype).indirect(offsets[:]))
+            return picked
 
         tab2_plane = zeroed_plane(TB, "tab2_plane")
         wc_plane = zeroed_plane(H, "wc_plane")
@@ -78,95 +117,58 @@ def tile_list_snail_pen_features_kernel(
         wo_plane = zeroed_plane(PASSES * N, "wo_plane")
         zero = keep.tile([P, 1], F32, name="zero")
         nc.scalar.activation(zero[:], zero_in[:], ACT.Silu)
-        load_packed_planes(nc.gpsimd, wc_plane, wc_scales)
+        load_shared_plane(nc.gpsimd, wc_plane, wc_scales)
         ident = keep.tile([P, P], F32, name="ident")
         make_identity(nc, ident[:])
 
-        raw = {}
-
-        def load_weight(w, key, chunk):
-            lo, hi = CHUNKS[chunk]
-            t = keep.tile([P, PASSES, PACK, P * (hi - lo)], F32, name="raw", tag="raw_%s%d" % (key, chunk % 2 if chunk < 4 else 2), align_bytes=64)
-            for a in range(PASSES):
-                rows = w[P * PACK * a : P * PACK * (a + 1), P * lo : P * hi]
-                nc.sync.dma_start(out=t[:, a], in_=rows.rearrange("(p j) c -> p j c", j=PACK))
-            for b in range(lo, hi):
-                raw[key, b] = t[:, :, :, P * (b - lo) : P * (b - lo + 1)]
-
-        wc = {}
-
-        def load_wc(chunk):
-            lo, hi = WC_CHUNKS[chunk]
-            t = keep.tile([P, PASSES, P * (hi - lo)], I32, name="wc%d" % chunk, align_bytes=64)
-            src = wc_words.rearrange("a p c i -> p a (c i)")[:, :, PACK * P * lo : PACK * P * hi]
-            nc.sync.dma_start(out=t[:], in_=src.bitcast(I32))
-            for b in range(lo, hi):
-                wc[b] = t[:, :, P * (b - lo) : P * (b - lo + 1)]
-
-        floor_t, page = {}, {}
-
-        def load_floor(b):
-            floor_t[b] = keep.tile([P, S], F32, name="floor", tag="floor%d" % b, align_bytes=64)
-            nc.sync.dma_start(out=floor_t[b][:], in_=floors[P * b : P * (b + 1), :])
-
-        def load_page(b):
-            page[b] = keep.tile([P, T2], F32, name="page", tag="wide%d" % b, align_bytes=64)
-            nc.sync.dma_start(out=page[b][:], in_=page0[P * b : P * (b + 1), :])
-
-        def load_gain(src, name):
-            t = keep.tile([P, S], F32, name=name)
-            nc.sync.dma_start(out=t[:], in_=src)
-            return t
-
         idx2 = load_list(offs2, "idx2")
-        tab2 = [load_words(tab2_words, a, "tab2", "wide%d" % (4 + a)) for a in range(PASSES)]
-        load_packed_planes(nc.sync, tab2_plane, tab2_scales)
+        tab2 = [load_words(tab2_words, a, "wide%d" % (TILES - 2 * PASSES + a)) for a in range(PASSES)]
+        load_shared_plane(nc.sync, tab2_plane, tab2_scales)
         load_wc(0)
-        tab = [load_words(tab_words, 0, "tab", "wide6")]
-        load_packed_planes(nc.sync, tab_plane, tab_scales)
+        tab = [load_words(tab_words, 0, "wide%d" % (TILES - PASSES))]
+        load_shared_plane(nc.sync, tab_plane, tab_scales)
         idx = load_list(offs, "idx")
-        tab.append(load_words(tab_words, 1, "tab", "wide7"))
-        load_weight(wd, "wd", 0)
-        load_weight(w1, "w1", 0)
+        tab.append(load_words(tab_words, 1, "wide%d" % (TILES - 1)))
+        load_weight("wd", 0)
+        load_weight("w1", 0)
         load_page(0)
         idx4 = load_list(offs4, "idx4")
         gain2 = load_gain(wg2, "gain2")
-        load_weight(wd, "wd", 1)
+        load_weight("wd", 1)
         load_floor(0)
         gain1 = load_gain(wg1, "gain1")
         idx3 = load_list(offs3, "idx3")
-        load_weight(w1, "w1", 1)
+        load_weight("w1", 1)
         idx5 = load_list(offs5, "idx5")
 
-        v2 = [gather(tab2[a], idx2, U32, "v2_%d" % a) for a in range(PASSES)]
-        v2_plane = gather(tab2_plane, idx2, U8, "v2_plane")
-        v = [gather(tab[a], idx, U32, "v%d" % a) for a in range(PASSES)]
-        v_plane = gather(tab_plane, idx, U8, "v_plane")
+        v2 = [gather_table(tab2[a], idx2, U32, "v2_%d" % a) for a in range(PASSES)]
+        v2_plane = gather_table(tab2_plane, idx2, U8, "v2_plane")
+        v = [gather_table(tab[a], idx, U32, "v%d" % a) for a in range(PASSES)]
+        v_plane = gather_table(tab_plane, idx, U8, "v_plane")
 
-        codes, planes = {}, {}
+        rounded, codes, planes = {}, {}, {}
 
-        grouped = {}
+        def rounded_buffer(key, b):
+            return "rounded_%s%d" % (key, b % DEPTH)
 
         def round_weight(key, b, copy):
-            grouped[key, b] = keep.tile(
-                [P, PASSES, P, PACK], BF16, name="grouped", tag="grouped_%s%d" % (key, b % 3), align_bytes=64
-            )
+            rounded[key, b] = held([P, PASSES, P, PACK], BF16, rounded_buffer(key, b))
             copy(
-                grouped[key, b][:].rearrange("p a (c i) t -> p a c t i", i=4),
+                rounded[key, b][:].rearrange("p a (c i) t -> p a c t i", i=4),
                 raw[key, b].rearrange("p a t (c i) -> p a c t i", i=4),
             )
 
-        def quantize_weight(key, b, after):
+        def quantize_weight(key, b, plane_buffer):
             codes[key, b] = ring3.tile([P, PASSES * P], U32, name="codes_" + key, align_bytes=64)
-            planes[key, b] = keep.tile([P, PASSES * P], U8, name="plane", tag=after, align_bytes=64)
+            planes[key, b] = held([P, PASSES * P], U8, plane_buffer)
             nc.vector.quantize_mx(
                 out=codes[key, b][:].bitcast(FP8X4),
                 scales=planes[key, b][:],
-                in_=grouped[key, b][:].rearrange("p a c t -> p (a c t)"),
+                in_=rounded[key, b][:].rearrange("p a c t -> p (a c t)"),
             )
 
-        def project(key, b, table, table_plane, tag):
-            acc = psum1.tile([P, BANK], F32, name=tag)
+        def project(key, b, table, table_plane, bank):
+            acc = psum1.tile([P, BANK], F32, name=bank)
             for a in range(PASSES):
                 cols = slice(P * a, P * (a + 1))
                 nc.tensor.matmul_mx(
@@ -180,33 +182,31 @@ def tile_list_snail_pen_features_kernel(
                 )
             return acc
 
-        h1_sum, h1, h2, cosine = {}, {}, {}, {}
-
-        def h1_tag(b):
-            return "wide%d" % (b - 1) if b else "h1_first"
-
-        def h2_tag(b):
-            return "grouped_wd%d" % ((b + 1) % 3) if b > 1 else ("grouped_w10", "h2_first")[b]
-
-        def make_h1(b):
-            acc = h1_sum[b]
-            h1[b] = keep.tile([P, S], F32, name="h1", tag=h1_tag(b), align_bytes=64)
-            nc.vector.tensor_tensor(h1[b][:], acc[:], floor_t[b][:], ALU.max)
-
         def add_transposed(bank, first, second):
-            blocks = BANK // P
+            blocks = bank.shape[1] // P
             for n, term in enumerate((first, second)):
-                for jt in range(blocks):
-                    cols = slice(P * jt, P * (jt + 1))
+                for block in range(blocks):
+                    cols = slice(P * block, P * (block + 1))
                     nc.tensor.matmul(
                         bank[:, cols], lhsT=term[:, cols], rhs=ident[:], is_transpose=True,
-                        start=(n == 0 and jt == 0), stop=(n == 1 and jt == blocks - 1),
+                        start=(n == 0 and block == 0), stop=(n == 1 and block == blocks - 1),
                     )
+
+        h1_sum, h1, h2, cosine = {}, {}, {}, {}
+
+        def h1_buffer(b):
+            return "wide%d" % (b - 1) if b else "h1_first"
+
+        def h2_buffer(b):
+            return rounded_buffer("wd", b + 1) if b > 1 else (rounded_buffer("w1", 0), "h2_second")[b]
+
+        def cosine_buffer(b):
+            return "cosine%d" % (b % DEPTH)
 
         def make_cosine(b):
             phase = psum1.tile([P, BANK], F32, name="bank_phase")
-            for jt in range(S // P):
-                cols = slice(P * jt, P * (jt + 1))
+            for block in range(S // P):
+                cols = slice(P * block, P * (block + 1))
                 for a in range(PASSES):
                     nc.tensor.matmul_mx(
                         out=phase[:, cols],
@@ -217,106 +217,112 @@ def tile_list_snail_pen_features_kernel(
                         start=(a == 0),
                         stop=(a == PASSES - 1),
                     )
-            turns = ring2.tile([P, S], F32, name="turns")[:]
-            shift = ring2.tile([P, S], F32, name="shift")[:]
-            nc.scalar.activation(turns, phase[:], ACT.Abs, bias=zero[:], scale=0.5 / math.pi)
+            turns = ring2.tile([P, S], F32, name="turns")
+            shift = ring2.tile([P, S], F32, name="shift")
             whole = ring2.tile([P, S], U32, name="whole")
-            nc.scalar.activation(whole[:], turns, ACT.Copy, bias=0.25)
-            nc.scalar.activation(shift, whole[:], ACT.Copy, bias=0.25, scale=-1.0)
+            nc.scalar.activation(turns[:], phase[:], ACT.Abs, bias=zero[:], scale=0.5 / math.pi)
+            nc.scalar.activation(whole[:], turns[:], ACT.Copy, bias=0.25)
+            nc.scalar.activation(shift[:], whole[:], ACT.Copy, bias=0.25, scale=-1.0)
             rest = psum1.tile([P, BANK], F32, name="bank_rest")
             add_transposed(rest[:], turns, shift)
-            cosine[b] = keep.tile([P, S], F32, name="cosine", tag="scratch%d" % (b % 3), align_bytes=64)[:]
-            nc.scalar.activation(cosine[b], rest[:], ACT.Sin, bias=zero[:], scale=2.0 * math.pi)
+            cosine[b] = held([P, S], F32, cosine_buffer(b))
+            nc.scalar.activation(cosine[b][:], rest[:], ACT.Sin, bias=zero[:], scale=2.0 * math.pi)
+
+        def make_h1(b):
+            h1[b] = held([P, S], F32, h1_buffer(b))
+            nc.vector.tensor_tensor(h1[b][:], h1_sum[b][:], floor[b][:], ALU.max)
 
         def make_h2(b):
             acc = project("wd", b, v2, v2_plane, "bank_d")
-            h2[b] = keep.tile([P, S], F32, name="h2", tag=h2_tag(b), align_bytes=64)
-            nc.vector.tensor_tensor(h2[b][:], acc[:], cosine[b], ALU.mult)
+            h2[b] = held([P, S], F32, h2_buffer(b))
+            nc.vector.tensor_tensor(h2[b][:], acc[:], cosine[b][:], ALU.mult)
 
         def put(b, values, gain, offsets):
             nc.vector.tensor_tensor(page[b][:].indirect(offsets[:]), values[:], gain[:], ALU.mult)
 
-        x = {}
-
-        def fetch(b, h0, h1, tag):
-            t = keep.tile([P, BANK * (h1 - h0)], F32, name="x", tag=tag, align_bytes=64)
-            nc.vector.tensor_copy(t[:], page[b][:].indirect(idx5[:, BANK * h0 // 16 : BANK * h1 // 16]))
-            for h in range(h0, h1):
-                x[b, h] = t[:, BANK * (h - h0) : BANK * (h - h0 + 1)]
+        def fetch(b, lo, hi, buffer):
+            x = held([P, hi - lo], F32, buffer)
+            nc.vector.tensor_copy(x[:], page[b][:].indirect(idx5[:, lo // LIST_ROWS : hi // LIST_ROWS]))
+            return x
 
         z_rows = {}
-        last_tanh = {}
 
-        def make_z(b, h, copy):
+        def store_z_rows(b, q, sums, copy):
             a, slot = divmod(b, PER_PASS)
             if slot == 0:
-                z_rows[a, h] = keep.tile([P, 4, 2, 2 * P], BF16, name="z_rows%d" % h, align_bytes=64)
-            xs = x[b, h]
-            if b == 0:
-                th = keep.tile([P, BANK], F32, name="th", tag="raw_wd0", align_bytes=64)
-            else:
-                th = ring2.tile([P, BANK], F32, name="th")
-            nc.scalar.activation(th[:], xs, ACT.Tanh, bias=zero[:])
-            last_tanh[0] = th
-            zt = psum2.tile([P, 4, P], F32, name="bank_z")
-            add_transposed(zt[:].rearrange("p j r -> p (j r)"), xs, th[:])
+                z_rows[a, q] = held([P, 2, 2, 2 * P], BF16, "z_rows%d" % q)
+            width = 2 * P // PER_PASS
             copy(
-                z_rows[a, h][:, :, :, 64 * slot : 64 * (slot + 1)].rearrange("p j u (q e) -> p j u q e", e=2),
-                zt[:].rearrange("p j (q u e) -> p j u q e", u=2, e=2),
+                z_rows[a, q][:, :, :, width * slot : width * (slot + 1)].rearrange("p i u (w e) -> p i u w e", e=2),
+                sums.rearrange("p i (w u e) -> p i u w e", u=2, e=2),
+            )
+
+        def make_z(b, x):
+            for h in range(HALVES):
+                x_half = x[:, BANK * h : BANK * (h + 1)]
+                if b == 0:
+                    tanh_x = held([P, BANK], F32, "raw_wd0")
+                else:
+                    tanh_x = ring2.tile([P, BANK], F32, name="tanh_x")
+                nc.scalar.activation(tanh_x[:], x_half, ACT.Tanh, bias=zero[:])
+                sums = psum2.tile([P, BANK // P, P], F32, name="bank_z")
+                add_transposed(sums[:].rearrange("p i r -> p (i r)"), x_half, tanh_x)
+                for k in range(2):
+                    store_z_rows(b, 2 * h + k, sums[:, 2 * k : 2 * k + 2, :], on_scalar)
+
+        def group_z(a, q, grouped, copy):
+            words = psum2.tile([P, 2, 2, P], F32, name="bank_w")
+            for i in range(2):
+                for u in range(2):
+                    nc.tensor.transpose(words[:, i, u, :], z_rows[a, q][:, i, u, :].bitcast(F32), ident[:])
+            copy(
+                grouped.bitcast(F32).rearrange("p (i j u) -> p i j u", i=2, u=2),
+                words[:].rearrange("p i u j -> p i j u"),
             )
 
         z_codes, z_plane = {}, {}
 
-        z_grouped = {}
+        def quantize_z(a, first_piece, grouped, codes_buffer):
+            width = grouped.shape[1] // PACK
+            made_codes = held([P, width], U32, codes_buffer)
+            made_plane = held([P, width], U8, "z_plane%d%d" % (a, first_piece))
+            nc.vector.quantize_mx(out=made_codes[:].bitcast(FP8X4), scales=made_plane[:], in_=grouped[:])
+            for k in range(width // PIECE):
+                z_codes[a, first_piece + k] = made_codes[:, PIECE * k : PIECE * (k + 1)]
+                z_plane[a, first_piece + k] = made_plane[:, PIECE * k : PIECE * (k + 1)]
 
-        def group_z(a, h, copies):
-            z_grouped[a, h] = ring2.tile([P, BANK * PACK], BF16, name="grouped_z", align_bytes=64)
-            words = z_grouped[a, h][:].bitcast(F32)
-            for k in range(2):
-                bank = psum2.tile([P, 2, 2, P], F32, name="bank_z" if (a, h) == (1, 1) else "bank_w")
-                for i in range(2):
-                    for u in range(2):
-                        nc.tensor.transpose(bank[:, i, u, :], z_rows[a, h][:, 2 * k + i, u, :].bitcast(F32), ident[:])
-                copies[k](
-                    words[:, BANK * k : BANK * (k + 1)].rearrange("p (i j u) -> p i j u", i=2, u=2),
-                    bank[:].rearrange("p i u j -> p i j u"),
-                )
-
-        def quantize_z(a, h, tag):
-            z_codes[a, h] = keep.tile([P, BANK], U32, name="z_codes", tag=tag, align_bytes=64)
-            z_plane[a, h] = keep.tile([P, BANK], U8, name="z_plane%d%d" % (a, h), align_bytes=64)
-            nc.vector.quantize_mx(out=z_codes[a, h][:].bitcast(FP8X4), scales=z_plane[a, h][:], in_=z_grouped[a, h][:])
-
-        def finish(h, nt, on_vector):
-            if nt < 2:
-                acc = psum1.tile([P, BANK], F32, name=(("bank_phase", "bank_rest"), ("bank_d", "bank_h"))[h][nt])
+        def finish(q, m):
+            if q < 2:
+                acc = psum1.tile([P, 2, PIECE], F32, name=(("bank_phase", "bank_rest"), ("bank_d", "bank_h"))[q][m])
             else:
-                acc = psum2.tile([P, BANK], F32, name=("bank_w", "bank_z")[h])
-            for a in range(PASSES):
+                acc = psum2.tile([P, 2, PIECE], F32, name=("bank_z", "bank_w")[q - 2])
+            steps = [(a, i, c) for a in range(PASSES) for i in range(2) for c in range(PIECE // P)]
+            for a, i, c in steps:
+                n0 = P * (2 * m + i)
+                cols = slice(P * c, P * (c + 1))
                 nc.tensor.matmul_mx(
-                    out=acc[:],
-                    lhsT=wo[:, a, 2 * P * nt : 2 * P * (nt + 1)].bitcast(FP4X4),
-                    lhsT_scale=wo_plane[:, N * a + P * nt : N * a + P * (nt + 1)],
-                    rhs=z_codes[a, h][:].bitcast(FP8X4),
-                    rhs_scale=z_plane[a, h][:],
-                    start=(a == 0),
-                    stop=(a == PASSES - 1),
+                    out=acc[:, i, cols],
+                    lhsT=wo[:, a, 2 * n0 : 2 * (n0 + P)].bitcast(FP4X4),
+                    lhsT_scale=wo_plane[:, N * a + n0 : N * a + n0 + P],
+                    rhs=z_codes[a, q][:, cols].bitcast(FP8X4),
+                    rhs_scale=z_plane[a, q][:, cols],
+                    start=(a, i, c) == steps[0],
+                    stop=(a, i, c) == steps[-1],
                 )
-            size = ring2.tile([P, BANK], F32, name="size", tag="turns" if on_vector else "whole")
-            if on_vector:
-                minus = ring2.tile([P, BANK], F32, name="minus", tag="th")
-                nc.vector.tensor_scalar(minus[:], acc[:], -1.0, None, ALU.mult)
-                nc.vector.tensor_tensor(size[:], acc[:], minus[:], ALU.max)
+            y = acc[:].rearrange("p i j -> p (i j)")
+            if q >= 2 and m == 0:
+                size = ring2.tile([P, BANK], F32, name="size", tag="turns")
+                minus = ring2.tile([P, BANK], F32, name="minus", tag="shift")
+                nc.vector.tensor_scalar(minus[:], y, -1.0, None, ALU.mult)
+                nc.vector.tensor_tensor(size[:], y, minus[:], ALU.max)
             else:
-                nc.scalar.activation(size[:], acc[:], ACT.Abs, bias=zero[:])
-            root = keep.tile([P, BANK], F32, name="root", tag="floor%d" % (4 * h + nt), align_bytes=64)
-            pieces = 2 if (h, nt) == (HALVES - 1, N // P - 1) else 1
-            for i in range(pieces):
-                lo, hi = BANK * i // pieces, BANK * (i + 1) // pieces
-                nc.scalar.activation(root[:, lo:hi], size[:, lo:hi], ACT.Sqrt, bias=zero_root[:])
-                nc.sync.dma_start(out=out[P * nt : P * (nt + 1), BANK * h + lo : BANK * h + hi], in_=root[:, lo:hi])
+                size = ring2.tile([P, BANK], F32, name="size", tag="whole")
+                nc.scalar.activation(size[:], y, ACT.Abs, bias=zero[:])
+            root = held([P, 2, PIECE], F32, "floor%d" % (2 * q + m))
+            nc.scalar.activation(root[:].rearrange("p i j -> p (i j)"), size[:], ACT.Sqrt, bias=zero_root[:])
+            rows = out[2 * P * m : 2 * P * (m + 1), PIECE * q : PIECE * (q + 1)]
+            nc.sync.dma_start(out=rows.rearrange("(i p) j -> p i j", i=2), in_=root[:])
 
-        on_scalar, on_vector = nc.scalar.copy, nc.vector.tensor_copy
         make_cosine(0)
         for key in ("wd", "w1"):
             round_weight(key, 0, on_vector)
@@ -327,17 +333,17 @@ def tile_list_snail_pen_features_kernel(
         round_weight("wd", 1, on_scalar)
         round_weight("w1", 1, on_scalar)
 
-        for chunk in range(2, len(CHUNKS)):
-            load_weight(wd, "wd", chunk)
-            load_weight(w1, "w1", chunk)
-            load_page(chunk - 1)
-            load_floor(chunk - 1)
-            if chunk == 2:
+        for load in range(2, len(WEIGHT_LOADS)):
+            load_weight("wd", load)
+            load_weight("w1", load)
+            load_page(load - 1)
+            load_floor(load - 1)
+            if load == 2:
                 load_wc(1)
-        for b in range(len(CHUNKS) - 1, TILES):
+        for b in range(len(WEIGHT_LOADS) - 1, TILES):
             load_page(b)
             load_floor(b)
-        wo = keep.tile([P, PASSES, 2 * N], U8, name="wo", align_bytes=64)
+        wo = held([P, PASSES, 2 * N], U8, "wo")
         nc.sync.dma_start(out=wo[:].bitcast(I32), in_=wo_words.rearrange("a p c -> p a c").bitcast(I32))
         for q in range(4):
             nc.sync.dma_start(
@@ -345,25 +351,26 @@ def tile_list_snail_pen_features_kernel(
                 in_=wo_scales[:, 4 * q : 4 * q + 4, :].rearrange("a r n -> r a n").bitcast(I32),
             )
 
+        first_pass = {}
         for b in range(TILES):
-            last = b == TILES - 1
             put(b, h2[b], gain2, idx4)
             make_h1(b)
             if b < 2:
-                quantize_weight("wd", b + 1, h2_tag(b))
+                quantize_weight("wd", b + 1, h2_buffer(b))
             if b == 1:
-                quantize_weight("wd", 3, "floor1")
+                quantize_weight("wd", b + 2, "floor%d" % b)
             if 2 <= b < TILES - 2:
-                quantize_weight("wd", b + 2, h2_tag(b))
+                quantize_weight("wd", b + 2, h2_buffer(b))
             if b >= TILES - HALVES:
-                quantize_z(0, b - (TILES - HALVES), h2_tag(b))
+                h = b - (TILES - HALVES)
+                quantize_z(0, 2 * h, first_pass[h], h2_buffer(b))
             put(b, h1[b], gain1, idx3)
-            if not last:
+            if b + 1 < TILES:
                 make_h2(b + 1)
-                quantize_weight("w1", b + 1, h1_tag(b))
+                quantize_weight("w1", b + 1, h1_buffer(b))
                 h1_sum[b + 1] = project("w1", b + 1, v, v_plane, "bank_h")
             if b == 0:
-                round_weight("wd", 2, on_scalar)
+                round_weight("wd", b + 2, on_scalar)
             if b + 3 < TILES:
                 round_weight("wd", b + 3, on_scalar)
             if b + 2 < TILES:
@@ -371,19 +378,28 @@ def tile_list_snail_pen_features_kernel(
                 make_cosine(b + 2)
             if b == PER_PASS:
                 for h in range(HALVES):
-                    group_z(0, h, (on_scalar, on_scalar))
-            if last:
-                fetch(b, 0, 1, "scratch0")
-                fetch(b, 1, 2, "scratch2")
-            else:
-                fetch(b, 0, 2, "scratch%d" % ((b + 1) % 3) if b > 1 else "grouped_w1%d" % (b + 1))
-            for h in range(HALVES):
-                make_z(b, h, on_vector if last else on_scalar)
+                    first_pass[h] = ring2.tile([P, BANK * PACK], BF16, name="first_pass", align_bytes=64)
+                    for k in range(2):
+                        group_z(0, 2 * h + k, first_pass[h][:, PIECE * PACK * k : PIECE * PACK * (k + 1)], on_scalar)
+            if b + 1 < TILES:
+                make_z(b, fetch(b, 0, J, cosine_buffer(b + 1) if b > 1 else rounded_buffer("w1", b + 1)))
+
+        last = TILES - 1
+        free = [cosine_buffer(0), cosine_buffer(2), rounded_buffer("w1", 2), rounded_buffer("wd", 0)]
+        x_last, tanh_last = [], []
+        for q in range(PIECES):
+            x_last.append(fetch(last, PIECE * q, PIECE * (q + 1), free[q]))
+            tanh_last.append(held([P, PIECE], F32, "wide%d" % q))
+            nc.scalar.activation(tanh_last[q][:], x_last[q][:], ACT.Tanh, bias=zero[:])
         zero_root = keep.tile([P, 1], F32, name="zero_root")
-        nc.scalar.activation(zero_root[:], last_tanh[0][:, :1], ACT.Sqrt, bias=zero[:], scale=0.0)
-        for h in range(HALVES):
-            group_z(1, h, (on_vector, on_scalar))
-            quantize_z(1, h, "wide%d" % h)
-        for h in range(HALVES):
-            for nt in range(N // P):
-                finish(h, nt, (h, nt) in {(0, 2), (0, 3), (1, 0), (1, 2)})
+        nc.scalar.activation(zero_root[:], tanh_last[-1][:, :1], ACT.Sqrt, bias=zero[:], scale=0.0)
+        for q in range(PIECES):
+            sums = psum2.tile([P, PIECE // P, P], F32, name="bank_z")
+            add_transposed(sums[:].rearrange("p i r -> p (i r)"), x_last[q], tanh_last[q])
+            store_z_rows(last, q, sums[:], on_vector)
+            grouped = held([P, PIECE * PACK], BF16, "raw_w1%d" % (q % 3))
+            group_z(1, q, grouped[:], on_vector)
+            quantize_z(1, q, grouped, "z_codes%d" % q)
+            for done in [q - 1] * (q > 0) + [q] * (q == PIECES - 1):
+                for m in range(2):
+                    finish(done, m)

import math
from contextlib import ExitStack

import concourse.mybir as mybir
from concourse.masks import make_identity

K, TA, TB, S, H, T2, J, N = 1024, 2048, 1024, 512, 1024, 2048, 1024, 512
FLOPS = 2 * (3 * K * H * S + H * N * J)

F32 = mybir.dt.float32
BF16 = mybir.dt.bfloat16
I32 = mybir.dt.int32
U32 = mybir.dt.uint32
U16 = mybir.dt.uint16
U8 = mybir.dt.uint8
FP8X4 = mybir.dt.float8_e4m3fn_x4
FP4X4 = mybir.dt.float4_e2m1fn_x4
ALU = mybir.AluOpType
ACT = mybir.ActivationFunctionType

P = 128
PACK = 4
PASSES = 2
BANK = 512
LIST_ROWS = 16
TILES = H // P
PER_PASS = TILES // PASSES
HALVES = J // BANK
PIECE = 256
PIECES = J // PIECE
DEPTH = 3
WEIGHT_LOADS = [(0, 1), (1, 2), (2, 4), (4, 6), (6, 8)]
WC_LOADS = [(0, DEPTH), (DEPTH, TILES)]


def tile_list_snail_pen_features_kernel(
    tc, tab_words, tab_scales, tab2_words, tab2_scales, offs, offs2, offs3, offs4, offs5,
    w1, floors, wc_words, wc_scales, wd, wg1, wg2, page0, wo_words, wo_scales, out,
):
    nc = tc.nc
    with ExitStack() as ctx:
        keep = ctx.enter_context(tc.tile_pool(name="keep", bufs=1))
        ring2 = ctx.enter_context(tc.tile_pool(name="ring2", bufs=2))
        ring3 = ctx.enter_context(tc.tile_pool(name="ring3", bufs=DEPTH))
        psum1 = ctx.enter_context(tc.psum_pool(name="psum1", bufs=1))
        psum2 = ctx.enter_context(tc.psum_pool(name="psum2", bufs=2))
        on_scalar, on_vector = nc.scalar.copy, nc.vector.tensor_copy

        def held(shape, dtype, buffer):
            return keep.tile(shape, dtype, name=buffer, align_bytes=64)

        def load_list(src, name):
            offsets = keep.tile(list(src.shape), U16, name=name)
            nc.sync.dma_start(out=offsets[:], in_=src)
            return offsets

        def load_words(src, a, buffer):
            words = held([P, src.shape[2]], I32, buffer)
            nc.sync.dma_start(out=words[:], in_=src[a].rearrange("p t i -> p (t i)").bitcast(I32))
            return words

        def zeroed_plane(width, buffer):
            plane = held([P, width], U8, buffer)
            nc.vector.memset(plane[:].bitcast(I32), 0)
            return plane

        def load_shared_plane(queue, plane, src):
            for q in range(4):
                queue.dma_start(
                    out=plane[32 * q : 32 * q + 4 * PASSES, :].bitcast(I32),
                    in_=src[:, 4 * q : 4 * q + 4, :].bitcast(I32),
                )

        raw, wc, floor, page = {}, {}, {}, {}

        def load_weight(key, load):
            lo, hi = WEIGHT_LOADS[load]
            slot = load % 2 if load < len(WEIGHT_LOADS) - 1 else 2
            staged = held([P, PASSES, PACK, P * (hi - lo)], F32, "raw_%s%d" % (key, slot))
            for a in range(PASSES):
                rows = {"w1": w1, "wd": wd}[key][P * PACK * a : P * PACK * (a + 1), P * lo : P * hi]
                nc.sync.dma_start(out=staged[:, a], in_=rows.rearrange("(p t) c -> p t c", t=PACK))
            for b in range(lo, hi):
                raw[key, b] = staged[:, :, :, P * (b - lo) : P * (b - lo + 1)]

        def load_wc(load):
            lo, hi = WC_LOADS[load]
            words = held([P, PASSES, P * (hi - lo)], I32, "wc%d" % load)
            src = wc_words.rearrange("a p c i -> p a (c i)")[:, :, PACK * P * lo : PACK * P * hi]
            nc.sync.dma_start(out=words[:], in_=src.bitcast(I32))
            for b in range(lo, hi):
                wc[b] = words[:, :, P * (b - lo) : P * (b - lo + 1)]

        def load_floor(b):
            floor[b] = held([P, S], F32, "floor%d" % b)
            nc.sync.dma_start(out=floor[b][:], in_=floors[P * b : P * (b + 1), :])

        def load_page(b):
            page[b] = held([P, T2], F32, "wide%d" % b)
            nc.sync.dma_start(out=page[b][:], in_=page0[P * b : P * (b + 1), :])

        def load_gain(src, name):
            gain = keep.tile([P, S], F32, name=name)
            nc.sync.dma_start(out=gain[:], in_=src)
            return gain

        def gather_table(window, offsets, dtype, buffer):
            picked = held([P, S], dtype, buffer)
            nc.vector.tensor_copy(picked[:], window[:].bitcast(dtype).indirect(offsets[:]))
            return picked

        tab2_plane = zeroed_plane(TB, "tab2_plane")
        wc_plane = zeroed_plane(H, "wc_plane")
        zero_in = keep.tile([P, 1], F32, name="zero_in")
        nc.vector.memset(zero_in[:], 0.0)
        tab_plane = zeroed_plane(TA, "tab_plane")
        wo_plane = zeroed_plane(PASSES * N, "wo_plane")
        zero = keep.tile([P, 1], F32, name="zero")
        nc.scalar.activation(zero[:], zero_in[:], ACT.Silu)
        load_shared_plane(nc.gpsimd, wc_plane, wc_scales)
        ident = keep.tile([P, P], F32, name="ident")
        make_identity(nc, ident[:])

        idx2 = load_list(offs2, "idx2")
        tab2 = [load_words(tab2_words, a, "wide%d" % (TILES - 2 * PASSES + a)) for a in range(PASSES)]
        load_shared_plane(nc.sync, tab2_plane, tab2_scales)
        load_wc(0)
        tab = [load_words(tab_words, 0, "wide%d" % (TILES - PASSES))]
        load_shared_plane(nc.sync, tab_plane, tab_scales)
        idx = load_list(offs, "idx")
        tab.append(load_words(tab_words, 1, "wide%d" % (TILES - 1)))
        load_weight("wd", 0)
        load_weight("w1", 0)
        load_page(0)
        idx4 = load_list(offs4, "idx4")
        gain2 = load_gain(wg2, "gain2")
        load_weight("wd", 1)
        load_floor(0)
        gain1 = load_gain(wg1, "gain1")
        idx3 = load_list(offs3, "idx3")
        load_weight("w1", 1)
        idx5 = load_list(offs5, "idx5")

        v2 = [gather_table(tab2[a], idx2, U32, "v2_%d" % a) for a in range(PASSES)]
        v2_plane = gather_table(tab2_plane, idx2, U8, "v2_plane")
        v = [gather_table(tab[a], idx, U32, "v%d" % a) for a in range(PASSES)]
        v_plane = gather_table(tab_plane, idx, U8, "v_plane")

        rounded, codes, planes = {}, {}, {}

        def rounded_buffer(key, b):
            return "rounded_%s%d" % (key, b % DEPTH)

        def round_weight(key, b, copy):
            rounded[key, b] = held([P, PASSES, P, PACK], BF16, rounded_buffer(key, b))
            copy(
                rounded[key, b][:].rearrange("p a (c i) t -> p a c t i", i=4),
                raw[key, b].rearrange("p a t (c i) -> p a c t i", i=4),
            )

        def quantize_weight(key, b, plane_buffer):
            codes[key, b] = ring3.tile([P, PASSES * P], U32, name="codes_" + key, align_bytes=64)
            planes[key, b] = held([P, PASSES * P], U8, plane_buffer)
            nc.vector.quantize_mx(
                out=codes[key, b][:].bitcast(FP8X4),
                scales=planes[key, b][:],
                in_=rounded[key, b][:].rearrange("p a c t -> p (a c t)"),
            )

        def project(key, b, table, table_plane, bank):
            acc = psum1.tile([P, BANK], F32, name=bank)
            for a in range(PASSES):
                cols = slice(P * a, P * (a + 1))
                nc.tensor.matmul_mx(
                    out=acc[:],
                    lhsT=codes[key, b][:, cols].bitcast(FP8X4),
                    lhsT_scale=planes[key, b][:, cols],
                    rhs=table[a][:].bitcast(FP8X4),
                    rhs_scale=table_plane[4 * a : P, :],
                    start=(a == 0),
                    stop=(a == PASSES - 1),
                )
            return acc

        def add_transposed(bank, first, second):
            blocks = bank.shape[1] // P
            for n, term in enumerate((first, second)):
                for block in range(blocks):
                    cols = slice(P * block, P * (block + 1))
                    nc.tensor.matmul(
                        bank[:, cols], lhsT=term[:, cols], rhs=ident[:], is_transpose=True,
                        start=(n == 0 and block == 0), stop=(n == 1 and block == blocks - 1),
                    )

        h1_sum, h1, h2, cosine = {}, {}, {}, {}

        def h1_buffer(b):
            return "wide%d" % (b - 1) if b else "h1_first"

        def h2_buffer(b):
            return rounded_buffer("wd", b + 1) if b > 1 else (rounded_buffer("w1", 0), "h2_second")[b]

        def cosine_buffer(b):
            return "cosine%d" % (b % DEPTH)

        def make_cosine(b):
            phase = psum1.tile([P, BANK], F32, name="bank_phase")
            for block in range(S // P):
                cols = slice(P * block, P * (block + 1))
                for a in range(PASSES):
                    nc.tensor.matmul_mx(
                        out=phase[:, cols],
                        lhsT=v2[a][:, cols].bitcast(FP8X4),
                        lhsT_scale=v2_plane[4 * a : P, cols],
                        rhs=wc[b][:, a, :].bitcast(FP8X4),
                        rhs_scale=wc_plane[4 * a : P, P * b : P * (b + 1)],
                        start=(a == 0),
                        stop=(a == PASSES - 1),
                    )
            turns = ring2.tile([P, S], F32, name="turns")
            shift = ring2.tile([P, S], F32, name="shift")
            whole = ring2.tile([P, S], U32, name="whole")
            nc.scalar.activation(turns[:], phase[:], ACT.Abs, bias=zero[:], scale=0.5 / math.pi)
            nc.scalar.activation(whole[:], turns[:], ACT.Copy, bias=0.25)
            nc.scalar.activation(shift[:], whole[:], ACT.Copy, bias=0.25, scale=-1.0)
            rest = psum1.tile([P, BANK], F32, name="bank_rest")
            add_transposed(rest[:], turns, shift)
            cosine[b] = held([P, S], F32, cosine_buffer(b))
            nc.scalar.activation(cosine[b][:], rest[:], ACT.Sin, bias=zero[:], scale=2.0 * math.pi)

        def make_h1(b):
            h1[b] = held([P, S], F32, h1_buffer(b))
            nc.vector.tensor_tensor(h1[b][:], h1_sum[b][:], floor[b][:], ALU.max)

        def make_h2(b):
            acc = project("wd", b, v2, v2_plane, "bank_d")
            h2[b] = held([P, S], F32, h2_buffer(b))
            nc.vector.tensor_tensor(h2[b][:], acc[:], cosine[b][:], ALU.mult)

        def put(b, values, gain, offsets):
            nc.vector.tensor_tensor(page[b][:].indirect(offsets[:]), values[:], gain[:], ALU.mult)

        def fetch(b, lo, hi, buffer):
            x = held([P, hi - lo], F32, buffer)
            nc.vector.tensor_copy(x[:], page[b][:].indirect(idx5[:, lo // LIST_ROWS : hi // LIST_ROWS]))
            return x

        z_rows = {}

        def store_z_rows(b, q, sums, copy):
            a, slot = divmod(b, PER_PASS)
            if slot == 0:
                z_rows[a, q] = held([P, 2, 2, 2 * P], BF16, "z_rows%d" % q)
            width = 2 * P // PER_PASS
            copy(
                z_rows[a, q][:, :, :, width * slot : width * (slot + 1)].rearrange("p i u (w e) -> p i u w e", e=2),
                sums.rearrange("p i (w u e) -> p i u w e", u=2, e=2),
            )

        def make_z(b, x):
            for h in range(HALVES):
                x_half = x[:, BANK * h : BANK * (h + 1)]
                if b == 0:
                    tanh_x = held([P, BANK], F32, "raw_wd0")
                else:
                    tanh_x = ring2.tile([P, BANK], F32, name="tanh_x")
                nc.scalar.activation(tanh_x[:], x_half, ACT.Tanh, bias=zero[:])
                sums = psum2.tile([P, BANK // P, P], F32, name="bank_z")
                add_transposed(sums[:].rearrange("p i r -> p (i r)"), x_half, tanh_x)
                for k in range(2):
                    store_z_rows(b, 2 * h + k, sums[:, 2 * k : 2 * k + 2, :], on_scalar)

        def group_z(a, q, grouped, copy):
            words = psum2.tile([P, 2, 2, P], F32, name="bank_w")
            for i in range(2):
                for u in range(2):
                    nc.tensor.transpose(words[:, i, u, :], z_rows[a, q][:, i, u, :].bitcast(F32), ident[:])
            copy(
                grouped.bitcast(F32).rearrange("p (i j u) -> p i j u", i=2, u=2),
                words[:].rearrange("p i u j -> p i j u"),
            )

        z_codes, z_plane = {}, {}

        def quantize_z(a, first_piece, grouped, codes_buffer):
            width = grouped.shape[1] // PACK
            made_codes = held([P, width], U32, codes_buffer)
            made_plane = held([P, width], U8, "z_plane%d%d" % (a, first_piece))
            nc.vector.quantize_mx(out=made_codes[:].bitcast(FP8X4), scales=made_plane[:], in_=grouped[:])
            for k in range(width // PIECE):
                z_codes[a, first_piece + k] = made_codes[:, PIECE * k : PIECE * (k + 1)]
                z_plane[a, first_piece + k] = made_plane[:, PIECE * k : PIECE * (k + 1)]

        def finish(q, m):
            if q < 2:
                acc = psum1.tile([P, 2, PIECE], F32, name=(("bank_phase", "bank_rest"), ("bank_d", "bank_h"))[q][m])
            else:
                acc = psum2.tile([P, 2, PIECE], F32, name=("bank_z", "bank_w")[q - 2])
            steps = [(a, i, c) for a in range(PASSES) for i in range(2) for c in range(PIECE // P)]
            for a, i, c in steps:
                n0 = P * (2 * m + i)
                cols = slice(P * c, P * (c + 1))
                nc.tensor.matmul_mx(
                    out=acc[:, i, cols],
                    lhsT=wo[:, a, 2 * n0 : 2 * (n0 + P)].bitcast(FP4X4),
                    lhsT_scale=wo_plane[:, N * a + n0 : N * a + n0 + P],
                    rhs=z_codes[a, q][:, cols].bitcast(FP8X4),
                    rhs_scale=z_plane[a, q][:, cols],
                    start=(a, i, c) == steps[0],
                    stop=(a, i, c) == steps[-1],
                )
            y = acc[:].rearrange("p i j -> p (i j)")
            if q >= 2 and m == 0:
                size = ring2.tile([P, BANK], F32, name="size", tag="turns")
                minus = ring2.tile([P, BANK], F32, name="minus", tag="shift")
                nc.vector.tensor_scalar(minus[:], y, -1.0, None, ALU.mult)
                nc.vector.tensor_tensor(size[:], y, minus[:], ALU.max)
            else:
                size = ring2.tile([P, BANK], F32, name="size", tag="whole")
                nc.scalar.activation(size[:], y, ACT.Abs, bias=zero[:])
            root = held([P, 2, PIECE], F32, "floor%d" % (2 * q + m))
            nc.scalar.activation(root[:].rearrange("p i j -> p (i j)"), size[:], ACT.Sqrt, bias=zero_root[:])
            rows = out[2 * P * m : 2 * P * (m + 1), PIECE * q : PIECE * (q + 1)]
            nc.sync.dma_start(out=rows.rearrange("(i p) j -> p i j", i=2), in_=root[:])

        make_cosine(0)
        for key in ("wd", "w1"):
            round_weight(key, 0, on_vector)
            quantize_weight(key, 0, "plane_first_" + key)
        make_h2(0)
        h1_sum[0] = project("w1", 0, v, v_plane, "bank_h")
        make_cosine(1)
        round_weight("wd", 1, on_scalar)
        round_weight("w1", 1, on_scalar)

        for load in range(2, len(WEIGHT_LOADS)):
            load_weight("wd", load)
            load_weight("w1", load)
            load_page(load - 1)
            load_floor(load - 1)
            if load == 2:
                load_wc(1)
        for b in range(len(WEIGHT_LOADS) - 1, TILES):
            load_page(b)
            load_floor(b)
        wo = held([P, PASSES, 2 * N], U8, "wo")
        nc.sync.dma_start(out=wo[:].bitcast(I32), in_=wo_words.rearrange("a p c -> p a c").bitcast(I32))
        for q in range(4):
            nc.sync.dma_start(
                out=wo_plane[32 * q : 32 * q + 4, :].bitcast(I32).rearrange("p (a n) -> p a n", a=PASSES),
                in_=wo_scales[:, 4 * q : 4 * q + 4, :].rearrange("a r n -> r a n").bitcast(I32),
            )

        first_pass = {}
        for b in range(TILES):
            put(b, h2[b], gain2, idx4)
            make_h1(b)
            if b < 2:
                quantize_weight("wd", b + 1, h2_buffer(b))
            if b == 1:
                quantize_weight("wd", b + 2, "floor%d" % b)
            if 2 <= b < TILES - 2:
                quantize_weight("wd", b + 2, h2_buffer(b))
            if b >= TILES - HALVES:
                h = b - (TILES - HALVES)
                quantize_z(0, 2 * h, first_pass[h], h2_buffer(b))
            put(b, h1[b], gain1, idx3)
            if b + 1 < TILES:
                make_h2(b + 1)
                quantize_weight("w1", b + 1, h1_buffer(b))
                h1_sum[b + 1] = project("w1", b + 1, v, v_plane, "bank_h")
            if b == 0:
                round_weight("wd", b + 2, on_scalar)
            if b + 3 < TILES:
                round_weight("wd", b + 3, on_scalar)
            if b + 2 < TILES:
                round_weight("w1", b + 2, on_scalar)
                make_cosine(b + 2)
            if b == PER_PASS:
                for h in range(HALVES):
                    first_pass[h] = ring2.tile([P, BANK * PACK], BF16, name="first_pass", align_bytes=64)
                    for k in range(2):
                        group_z(0, 2 * h + k, first_pass[h][:, PIECE * PACK * k : PIECE * PACK * (k + 1)], on_scalar)
            if b + 1 < TILES:
                make_z(b, fetch(b, 0, J, cosine_buffer(b + 1) if b > 1 else rounded_buffer("w1", b + 1)))

        last = TILES - 1
        free = [cosine_buffer(0), cosine_buffer(2), rounded_buffer("w1", 2), rounded_buffer("wd", 0)]
        x_last, tanh_last = [], []
        for q in range(PIECES):
            x_last.append(fetch(last, PIECE * q, PIECE * (q + 1), free[q]))
            tanh_last.append(held([P, PIECE], F32, "wide%d" % q))
            nc.scalar.activation(tanh_last[q][:], x_last[q][:], ACT.Tanh, bias=zero[:])
        zero_root = keep.tile([P, 1], F32, name="zero_root")
        nc.scalar.activation(zero_root[:], tanh_last[-1][:, :1], ACT.Sqrt, bias=zero[:], scale=0.0)
        for q in range(PIECES):
            sums = psum2.tile([P, PIECE // P, P], F32, name="bank_z")
            add_transposed(sums[:].rearrange("p i r -> p (i r)"), x_last[q], tanh_last[q])
            store_z_rows(last, q, sums[:], on_vector)
            grouped = held([P, PIECE * PACK], BF16, "raw_w1%d" % (q % 3))
            group_z(1, q, grouped[:], on_vector)
            quantize_z(1, q, grouped, "z_codes%d" % q)
            for done in [q - 1] * (q > 0) + [q] * (q == PIECES - 1):
                for m in range(2):
                    finish(done, m)
